import numpy as np, ml_dtypes
CORES = [9,25,41,57]
N = 4
BF = ml_dtypes.bfloat16
def gentries(a):
    return np.ascontiguousarray(a.reshape(8, 16, -1).transpose(0, 2, 1)).reshape(8, -1)
def gtable(e):
    e = np.asarray(e); return np.ascontiguousarray(e.reshape(8, -1, 16).transpose(0, 2, 1)).reshape(128, -1).astype(np.int32)
E, V, XB, K0, RO = 4096, 2048, 6, 4, 2
MASKS = [1, 2]
C, TOP, OFF = 2 ** K0, 2 ** XB - 1, 64 * 2 ** XB
def cut(rng, n, m):
    return np.repeat(np.arange(len(n)), n)[:m][rng.permutation(m)]
def ring(rng, cid):
    o = np.lexsort((rng.random(E), cid)); c = cid[o]
    st = np.flatnonzero(np.concatenate([np.array([True]), c[1:] != c[:-1]])); n = np.diff(np.append(st, E))
    nx = np.arange(1, E + 1); nx[np.append(st[1:], E) - 1] = st
    s, l, p = np.empty(E, np.int64), np.empty(E, np.int64), np.empty(E, np.int64)
    s[o] = o[nx]; l[o] = np.repeat(np.minimum.reduceat(o, st), n); p[o] = np.arange(E) - np.repeat(st, n)
    return s, l, p
def rings(rng, cid):
    s, l, p = np.empty(cid.shape, np.int64), np.empty(cid.shape, np.int64), np.empty(cid.shape, np.int64)
    for q in range(N):
        for g in range(8): s[q, g], l[q, g], p[q, g] = ring(rng, cid[q, g])
    return s, l, p
def deal(rng):
    return np.stack([np.stack([cut(rng, np.append(C, rng.integers(1, C + 1, E)), E) for g in range(8)]) for q in range(N)])
def levels(rng, l):
    w = rng.random((N, 8, 16, 1)); lev = np.take_along_axis(rng.random((N, 8, 16, E)), l[:, :, None, :], 3)
    return np.minimum((2 ** XB * (w * lev + (1 - w) * rng.random((N, 8, 16, E)))).astype(np.int64), TOP)
def chains(rng):
    n = 5 * V // 16; o = np.sort(np.append(0, 1 + rng.permutation(V - 1))[:3 * n].reshape(n, 3), axis=1); d = 2 * o + rng.integers(0, 2, (n, 3)); c = np.arange(E)
    c[d[:, 0]] = d[:, 1]; c[d[:, 0] ^ 1] = d[:, 2]
    return c
def graded(rng):
    o = rng.permutation(V); n = V // 8; c = np.arange(E); x = np.zeros((16, E), np.int64)
    a, b, d = o[:n], o[n:2 * n], o[2 * n:3 * n]; c[2 * a] = 2 * d; c[2 * a + 1] = 2 * b; c[2 * b + 1] = 2 * d + 1
    y = rng.integers(2 ** (XB - 1) + 1, TOP, (16, n)); up = rng.integers(0, 2, (16, n)); up[0] = 1
    x[:, 2 * d] = y + up; x[:, 2 * b + 1] = y; x[:, 2 * a + 1] = TOP
    a, b = o[3 * n::2], o[3 * n + 1::2]; c[2 * a + 1] = 2 * b
    y = rng.integers(2 ** (XB - 1) + 1, TOP, (16, len(a))); up = rng.integers(0, 2, y.shape); up[0] = 1
    x[:, 2 * a] = y; x[:, 2 * b + 1] = y + up
    return c, x
def pack(x, s, l):
    return {"x0": np.ascontiguousarray(x.reshape(N, 128, E)).astype(np.float32).astype(BF), "su": np.stack([gtable(a) for a in s]), "lab": l.astype(np.int32)}
def setup_inputs(rng):
    s, l, p = rings(rng, deal(rng))
    return pack(levels(rng, l), s, l)
def setup_inputs_full(rng):
    cid = np.empty((N, 8, E), np.int64); n = E // C
    for q in range(N):
        for g in range(8):
            if g & 1: cid[q, g] = cut(rng, np.full(n, C), E); continue
            c = np.full(E, -1, np.int64); top = V - 1
            for t in range(RO):
                w = 2 ** (t + 1); k = np.arange(n // w); flip = rng.integers(0, 2, len(k)); e = 2 * (top - k)
                c[e + flip] = w * k + rng.integers(0, w // 2, len(k)); c[e + 1 - flip] = w * k + w // 2 + rng.integers(0, w // 2, len(k)); top -= n // w
            free = np.repeat(np.arange(n), C - np.bincount(c[c >= 0], minlength=n))
            c[c < 0] = rng.permutation(free); cid[q, g] = c
    s, l, p = rings(rng, cid); x = levels(rng, l); x[:, ::2] = rng.integers(1, TOP + 1, (1, 4, 1, 1))
    return pack(x, s, l)
def setup_inputs_ties(rng):
    cid = deal(rng)
    cid[0, 0] = cut(rng, np.full(E // C, C), E)
    cid[0, 1, 0::2] = 2 * cut(rng, rng.integers(1, C + 1, V), V); cid[0, 1, 1::2] = 2 * cut(rng, rng.integers(1, C + 1, V), V) + 1
    cid[0, 1, 0] = E; cid[0, 1, 1] = E + 1
    for q in range(N): cid[q, 4] = chains(rng)
    cid[0, 6], lev = graded(rng)
    s, l, p = rings(rng, cid)
    for a in (s, l, p): a[:, [0, 1, 6]] = a[0:1, [0, 1, 6]].copy()
    x = TOP * rng.integers(0, 2, (N, 8, 16, E))
    x[:, 0] = TOP * (p[:, 0, None, :] & 1); x[:, 1] = TOP * (1 - (np.arange(E) & 1))
    x[:, 2:4] = rng.integers(0, 2, (N, 2, 16, E)); x[:, 4:6] = rng.integers(0, TOP + 1, (N, 2, 1, 1)); x[:, 6] = lev
    return pack(x, s, l)
def setup_inputs_ends(rng):
    cid = deal(rng); e = np.arange(E)
    shut = rng.permutation(np.concatenate([np.array([0, 7]), 1 + rng.permutation(6)])[:N]); z = int(rng.choice(np.flatnonzero(shut < 7)))
    for q in range(N):
        k = rng.permutation(8); i = int(np.flatnonzero(k == 3)[0]); k[i] = k[shut[q]]; k[shut[q]] = 3
        if q == z: k = np.where(k == 3, 3, 0); k[7] = 7
        for g in range(8):
            if k[g] == 0: cid[q, g] = e
            if k[g] in (1, 2, 3, 6): cid[q, g] = np.repeat(cut(rng, rng.integers(1, C // 2 + 1, V), V), 2)
            if k[g] == 1: cid[q, g, 0] = E; cid[q, g, 1] = E + 1
            if k[g] == 2: cid[q, g, E - 2] = E; cid[q, g, E - 1] = E + 1
            if k[g] == 4: cid[q, g] = cut(rng, np.full(E // C, C), E)
            if k[g] == 5: cid[q, g] = ((e + 1) >> 1) & (V - 1)
            if k[g] == 6: cid[q, g, V:] = E + cut(rng, rng.integers(1, C + 1, V), V)
    s, l, p = rings(rng, cid)
    return pack(levels(rng, l), s, l)
def setup_inputs_spread(rng):
    cid = np.stack([np.stack([cut(rng, np.minimum(np.exp2((K0 + 1) * rng.random(E)).astype(np.int64), C), E) for g in range(8)]) for q in range(N)])
    s, l, p = rings(rng, cid)
    x = np.exp2((XB + 1) * rng.random((N, 8, 1, E))) * rng.random((N, 8, 16, E)) * (rng.random((N, 8, 1, E)) > 0.0625)
    return pack(np.minimum(x.astype(np.int64), TOP), s, l)
def check_inputs(d):
    bad = []; x = np.asarray(d["x0"]).astype(np.float32)
    if not np.all((x >= 0) & (x <= TOP) & (x == np.floor(x))): bad.append("range of x0")
    if np.min(d["su"]) < 0 or np.max(d["su"]) >= E: return bad + ["range of su"]
    s = np.stack([gentries(a) for a in d["su"]]).astype(np.int64); e = np.broadcast_to(np.arange(E), s.shape)
    if not np.array_equal(np.sort(s, axis=2), e): bad.append("su is no permutation")
    cur, low, back = e, e, np.zeros(s.shape, bool)
    for t in range(C):
        cur = np.take_along_axis(s, cur, 2); low = np.minimum(low, cur); back = back | (cur == e)
    if not np.all(back): bad.append("a circuit of su is too long")
    if not np.array_equal(low, np.asarray(d["lab"])): bad.append("lab is not the lowest edge of the circuit")
    return bad
def reference(x0, su, lab):
    x = x0.astype(np.float32).astype(np.int64).reshape(N, 8, 16, E)
    s = np.stack([gentries(a) for a in su]).astype(np.int64); l = lab.astype(np.int64); v = np.arange(V)
    for t in range(RO):
        K = K0 + t; gain = np.zeros((N, 8, V), np.int64)
        for y in (x, x[np.arange(N) ^ MASKS[t]]):
            o = np.take_along_axis(y, s[:, :, None, :], 3)
            i0, i1, o0, o1 = y[..., 0::2], y[..., 1::2], o[..., 0::2], o[..., 1::2]
            gain = gain + np.add.reduce(np.abs(i0 - o0) + np.abs(i1 - o1) - np.abs(i0 - o1) - np.abs(i1 - o0), axis=2)
        l0, l1 = l[..., 0::2], l[..., 1::2]
        key = np.where(l0 != l1, V * (gain + OFF) + v, 0)
        b, a, j = np.repeat(key, 2, axis=2), x, s
        for k in range(K):
            a = a + np.take_along_axis(a, j[:, :, None, :], 3)
            b = np.maximum(b, np.take_along_axis(b, j, 2))
            j = np.take_along_axis(j, j, 2)
        merge = (key > 0) & (b[..., 0::2] == key) & (b[..., 1::2] == key)
        s0, s1 = s[..., 0::2], s[..., 1::2]
        s = np.stack([np.where(merge, s1, s0), np.where(merge, s0, s1)], axis=3).reshape(N, 8, E)
        low = np.where(merge, np.minimum(l0, l1), E)
        l = np.where(b > 0, np.minimum(l, np.take_along_axis(low, b & (V - 1), 2)), l)
        x = a >> K
    return {"ysu": s.astype(np.float32), "ylab": l.astype(np.float32), "yx": x.reshape(N, 128, E).astype(np.float32).astype(BF)}

from concourse.mybir import AluOpType, ActivationFunctionType

E = 4096
C = 256
CH = 1024
NCH = E // CH
MASKS = [1, 2]
K0 = 4
XOFF = 160.0
SHARE = (3, 4)
NS = 2
JV = ((1, 0, 3), (1, 1, 3), (1, 3, 3))
UPJ = 2000
PM = (1, 1, 1, 2, 4, 5, 5, 10)
TA = 2
TL = 2
EST = {"gather": 1.3e-3, "cycle": 1.0e-3, "pe": 0.5e-3, "dma": 2.0, "bw": 200e3, "rbw": 40e3, "look": 0.3, "small": 0.8}

SCRATCH = {}
for _names, _cols, _dt in (
        ("xa xb xc aa ab ob ma mb j0 ja jb", E, "bfloat16"), ("af w0 wa wb uu olab", E, "float32"),
        ("sui labi bi vi hii loi", C, "int32"), ("digi", 2 * C, "int32"),
        ("dig0 dig1 ddig md td", 2 * C, "bfloat16"), ("eqq", 128, "bfloat16"), ("eqt nw cfr k1", C, "bfloat16"),
        ("own0 par0 par1 jt0 jt1 jt2 jt3 jt4", 2 * C, "uint16"), ("own1 hs0 hs1 hr0 hr1 lsu llab", C, "uint16"),
        ("hpe tk bk bt lt zt vf suf t1 t2 t3 t4 cc efr pos", C, "float32"),
        ("kk ki", 4, "int32"), ("kf c7 cdp cdq ce ch cr cp", 4, "float32"),
        ("dif sf", 128, "float32"), ("yh", 144, "float32"), ("zn zr zs zm ze", 144, "bfloat16"),
        ("i1 m1 i16 ie s1 s16 p2", 128, "bfloat16")):
    for _n in _names.split():
        SCRATCH[_n] = ("sbuf", [128, _cols], _dt)
PSUM = {"pa": 2048, "pj": 1024, "pg": 512, "ph": 512}
for _n in PSUM:
    SCRATCH[_n] = ("psum", [128, PSUM[_n]], "float32")
NDMA = 80
SEMAPHORES = (["qv", "qa", "qp", "qg", "left"] + ["d%d" % i for i in range(NDMA)] + ["r%d" % i for i in range(6)])


def rank_program(g, core, T, topo):
    rank = T.rank_of(core)
    if rank is None:
        return
    A = AluOpType
    F = ActivationFunctionType
    eng = {"v": g.vector, "a": g.scalar, "p": g.tensor, "g": g, "s": g.sync}
    ops = []
    up = [0]

    def ap(name, lo=0, hi=None, step=1, row=None):
        t = T[name]
        if hi is None:
            hi = SCRATCH[name][1][1]
        cols = slice(lo, hi) if step == 1 else slice(lo, hi, step)
        n = len(range(lo, hi, step))
        if row == "both":
            return t[0:128:8, cols], (name, lo, hi, None), n / 8
        a = t[:, cols] if row is None else t[row:128:16, cols]
        if name in PSUM:
            return a, (name, lo // 512 * 512, (hi + 511) // 512 * 512, None), n
        return a, (name, lo, hi, row), n if row is None else n / 16

    def wide(a):
        return 2 if SCRATCH[a[1][0]][2] in ("bfloat16", "uint16") else 4

    def op(q, fn, reads, writes, kind="c", token=None, how=None):
        busy, late = 0.0, 0.0
        if kind == "d":
            side = (reads + writes)[0]
            busy, late = (1.0 if q == "g" else 0.1), EST["dma"] + 128 * side[2] * wide(side) / EST["bw"]
        elif kind == "r":
            busy, late = 1.0, EST["dma"] + 128 * reads[0][2] * 2 / EST["rbw"]
        elif how == "gather":
            busy = 0.06 + EST["gather"] * writes[0][2]
        elif q == "p":
            busy, late = max(64, reads[1][2]) * (1 if wide(reads[1]) == 2 else 4) * EST["pe"], 0.15
        elif q == "a":
            busy = 0.1 + EST["cycle"] * writes[0][2]
        elif q == "g":
            busy = 0.15 + 2 * EST["cycle"] * writes[0][2]
        elif q == "v":
            k = 0.5 if all(wide(a) == 2 for a in reads[:2 if how else 1] + writes) else 1.0
            if how == "two" and not any(a[1][0] in PSUM for a in reads):
                k *= 2
            busy = 0.06 + EST["cycle"] * max(64, k * writes[0][2])
        ops.append({"q": q, "up": up[0], "busy": busy, "late": late + 0.1, "fn": fn,
                    "r": [r[1] for r in reads if r[1][0] not in PSUM],
                    "w": [w[1] for w in writes] + [r[1] for r in reads if r[1][0] in PSUM],
                    "kind": kind, "token": token, "sig": False,
                    "full": all(w[1][0] in PSUM or w[1][3] is not None or w[2] == w[1][2] - w[1][1] for w in writes)})

    def col(name, j=0):
        return ap(name, j, j + 1)

    def ts(out, in0, s1, s2, op0, op1=None):
        rd = [in0] + [s for s in (s1, s2) if isinstance(s, tuple)]
        a1 = s1[0] if isinstance(s1, tuple) else s1
        a2 = s2[0] if isinstance(s2, tuple) else s2
        if op1 is None:
            op("v", lambda: g.vector.tensor_scalar(out[0], in0[0], a1, None, op0), rd, [out])
        else:
            op("v", lambda: g.vector.tensor_scalar(out[0], in0[0], a1, a2, op0, op1), rd, [out])

    def tt(out, in0, in1, o):
        op("v", lambda: g.vector.tensor_tensor(out[0], in0[0], in1[0], o), [in0, in1], [out], how="two")

    def cp(out, in_):
        op("v", lambda: g.vector.tensor_copy(out[0], in_[0]), [in_], [out])

    def act(out, in_, scale=1.0, bias=0.0, func=F.Identity):
        rd = [in_] + [s for s in (scale, bias) if isinstance(s, tuple)]
        sc = scale[0] if isinstance(scale, tuple) else scale
        bi = bias[0] if isinstance(bias, tuple) else bias
        op("a", lambda: g.scalar.activation(out[0], in_[0], func, bias=bi, scale=sc), rd, [out])

    def mm(out, lhs, rhs, start, stop):
        op("p", lambda: g.tensor.matmul(out[0], lhs[0], rhs[0], start, stop), [lhs, rhs], [out])

    def piece(name, i, n=1):
        return ap(name, i * CH, (i + n) * CH)

    def offs(tab, base, i, n=1):
        return ap(tab, base + i * CH // 16, base + (i + n) * CH // 16)

    def vgather(out, win, tab, base, i, in1, o):
        w, f, d, b = ap(win), offs(tab, base, i), piece(out, i), piece(in1, i)
        op("v", lambda: g.vector.tensor_tensor(d[0], w[0].indirect(f[0]), b[0], o), [w, f, b], [d], how="gather")

    def agather(out, win, tab, base, i, scale=1.0, bias=0.0):
        w, f, d = ap(win), offs(tab, base, i), piece(out, i)
        op("a", lambda: g.scalar.activation(d[0], w[0].indirect(f[0]), F.Identity, bias=bias, scale=scale), [w, f], [d],
           how="gather")

    ndma = [0]

    def dma(out, in_, q="s"):
        s = "d%d" % ndma[0]
        ndma[0] += 1
        op(q, lambda: eng[q].dma_start(out[0], in_[0]), [in_] if in_[1] else [], [out] if out[1] else [], "d", (s, 16))

    nsend = [0]
    left = [0]

    def exchange(t, land, src):
        dst = T.cores[rank ^ MASKS[t]]
        rid, pid, _ = topo.addr(dst)
        s = "r%d" % nsend[0]
        nsend[0] += 1
        left[0] += len(topo.engines(core, dst))
        op("g", lambda: g.remote_dma(land[0], src[0], T.sem[s], T.sem.left, pid, rid, topo.mask(core, dst)), [src], [], "r")
        op(None, None, [], [land], "x", (s, len(topo.engines(dst, core))))

    def iota(out, pattern, base, mult, flag=True, behind=()):
        if flag:
            op("g", lambda: g.iota(out[0], pattern, base, mult, allow_small_or_imprecise_dtypes=True), list(behind), [out])
        else:
            op("g", lambda: g.iota(out[0], pattern, base, mult), [], [out])

    def mark(name, base, fill):
        o = ap(name, 15, 144, 16)
        op("g", lambda: g.affine_select(o[0], o[0], [[-16, 9]], A.not_equal, fill, base, 1), [o], [o])

    def band(name, s):
        return ap(name, s, s + 128)

    dma(ap("sui"), (T.su[:], None))
    dma(ap("labi"), (T.lab[:], None), "a")
    dma(ap("xa"), (T.x0[:], None))
    dma(piece("xc", 0), (T.x0[:, 0:CH], None))
    dma(piece("xc", 1, 3), (T.x0[:, CH:E], None))
    for nm, lo, hi in (("zn", 0, 144), ("zr", 0, 144), ("j0", 0, 1400), ("j0", 1400, 2800), ("j0", 2800, E)):
        o = ap(nm, lo, hi)
        op("v", lambda o=o: g.vector.memset(o[0], 0.0), [], [o])
    iota(col("kk"), [[0, 1]], 0, 1, False)
    iota(ap("dif"), [[1, 128]], 0, -1)
    iota(ap("yh"), [[1, 72], [0, 2]], 0, 0)
    mark("zr", 0, 1.0)
    mark("zr", -1, 256.0)
    mark("zn", 0, 16.0)
    mark("zn", -1, 1.0)
    iota(ap("cc"), [[1, C]], 0, 0)
    cp(ap("own0", 0, C), ap("sui"))
    exchange(0, ap("par0", 0, C), ap("own0", 0, C))
    ts(ap("digi", 0, C), ap("sui"), 4, None, A.arith_shift_right)
    ts(ap("digi", C, 2 * C), ap("sui"), 15, None, A.bitwise_and)
    tt(ap("eqq"), ap("labi", 0, C, 2), ap("labi", 1, C, 2), A.is_equal)
    cp(ap("dig0"), ap("digi"))
    dma(ap("j0", row=0), ap("dig0", 0, C))
    dma(ap("j0", row=1), ap("dig0", C, 2 * C))
    dma(ap("j0", 0, E // 2, row=2), ap("eqq"))
    ts(col("ki", 0), col("kk"), 4, None, A.arith_shift_right)
    ts(col("ki", 1), col("kk"), 15, None, A.bitwise_and)
    ts(col("ki", 2), col("kk"), 1, None, A.arith_shift_right)
    ts(col("ki", 3), col("kk"), 1, None, A.bitwise_and)
    ts(ap("i1"), ap("dif"), 0.0, None, A.is_equal)
    cp(ap("kf"), ap("ki"))
    ts(col("cdp"), col("kf", 3), -2.0, 1.0, A.mult, A.add)
    ts(col("c7"), col("kf", 0), 8.0, 7.0, A.mult, A.add)
    ts(col("ce"), col("kf", 1), 2.0, -8192.0, A.is_equal, A.mult)
    ts(ap("s1"), ap("dif"), col("cdp"), None, A.is_equal)
    ts(ap("zs"), ap("yh"), col("c7"), None, A.is_equal)
    ts(ap("s16"), ap("dif"), col("cdp"), 16.0, A.is_equal, A.mult)
    act(ap("cfr"), ap("cc"), 1.0 / 256)
    act(ap("k1"), ap("cc"), 0.0, 1024.0)
    act(col("cr"), col("kf", 1), 1.0 / 4096)
    act(col("ch"), col("kf", 1), 1.0 / 4096, 1024.0)
    act(ap("efr"), ap("cc"), 1.0 / 256, col("cr"))
    mm(ap("ph", 0, C), ap("s16"), ap("dig0", 0, C), True, False)
    mm(ap("ph", 0, C), ap("s1"), ap("dig0", C, 2 * C), False, True)

    def reduce_piece(ps, z, m, i, close):
        for r in range(16):
            mm(ap(ps, i * 64, i * 64 + 64), band(z, 14 - r // 2 * 2), ap(m, i * CH + r, (i + 1) * CH, 16),
               False, close and r == 15)

    def lists_piece(j, i, both):
        for r in range(4 * i, 4 * i + 4) if both else ():
            mm(ap("pj", C, 2 * C), band("zn", 15 - r), ap(j, r * C, (r + 1) * C), r == 0, r == 15)
        for r in range(16):
            mm(ap("pj", 2 * C + i * 64, 2 * C + i * 64 + 64), band("zr", 15 - r), ap(j, i * CH + r, (i + 1) * CH, 16),
               r == 0, r == 15)

    def first_list():
        for r in range(16):
            mm(ap("pj", 2 * C, 3 * C), band("zr", 15 - r), ap("j0", r, E, 16), r == 0, r == 15)

    def add_piece(a, i):
        for h in range(2):
            lo = i * CH + h * 512
            o = ap("pa", i % 2 * CH + h * 512, i % 2 * CH + h * 512 + 512)
            mm(o, ap("i1"), ap(a, lo, lo + 512), True, False)
            mm(o, ap("i1"), ap("ob", lo, lo + 512), False, True)

    def add_turned(a, h):
        for r in range(2 * h, 2 * h + 2):
            o = ap("pa", r % 8 * C, (r % 8 + 1) * C)
            mm(o, ap("i1"), ap(a, r, E, 16), True, False)
            mm(o, ap("i1"), ap("ob", r, E, 16), False, True)

    def evac_turned(out, i):
        for r in range(4 * i, 4 * i + 4):
            act(ap(out, r, E, 16), ap("pa", r % 8 * C, (r % 8 + 1) * C))

    def evac(out, i, scale, bias):
        act(piece(out, i), ap("pa", i % 2 * CH, i % 2 * CH + CH), scale, bias)

    def first_evac(x, i, bias, na):
        if i < 2:
            for h in (2 * i, 2 * i + 1):
                act(ap("aa", h * 512, h * 512 + 512), ap("pa", h * 512, h * 512 + 512), 1.0, bias)
                add_turned(x, h + 4)
        else:
            evac("aa", i, 1.0, bias)
        if i >= na:
            dma(piece("ab", i), piece("aa", i))

    def scalar_gains(x, i):
        lo = i * CH

        def differences():
            for h in range(2):
                o = ap("pa", h * 512, h * 512 + 512)
                mm(o, ap("i1"), ap(x, lo + h * 512, lo + h * 512 + 512), True, False)
                mm(o, ap("m1"), ap("ob", lo + h * 512, lo + h * 512 + 512), False, True)
            for h in range(2):
                o = ap("pa", CH + h * 512, CH + h * 512 + 512)
                mm(o, ap("i1"), ap(x, lo + 1 - h, lo + CH, 2), True, False)
                mm(o, ap("m1"), ap("ob", lo + h, lo + CH, 2), False, True)

        def clip():
            act(piece("ab", i), ap("pa", 0, CH), func=F.Relu)
            act(piece("ab", i - 2), ap("pa", CH, 2 * CH), func=F.Relu)

        def total():
            reduce_piece("pg", "zs", "ab", i, False)
            for h in range(2):
                for u in range(8):
                    b = (i - 2) * CH + h * 512
                    mm(ap("pg", i * 64, i * 64 + 64), band("zm", 14 - 2 * u), ap("ab", b + u, b + 512, 8), False, False)
        return differences, clip, total

    now = [0]
    jw = ["j0", "ja", "jb", "ja", "jb"]
    ww = ["w0", "wa", "wb", "wa", "wb", "wa"]

    def jstep(k, i, lists=True):
        if (now[0], k, i) in JV:
            w, f, d = ap(jw[k]), offs("jt%d" % k, C, i), piece(jw[k + 1], i)
            up[0] = UPJ
            op("v", lambda: g.vector.tensor_copy(d[0], w[0].indirect(f[0])), [w, f], [d], how="gather")
            up[0] = 0
        else:
            agather(jw[k + 1], jw[k], "jt%d" % k, C, i)
        if lists:
            lists_piece(jw[k + 1], i, k >= 2)

    def jconv(k):
        if k >= 3:
            cp(ap("jt%d" % k), ap("pj", C, 3 * C))
        else:
            cp(ap("jt%d" % k, C, 2 * C), ap("pj", 2 * C, 3 * C))

    def astep(k, src, dst, scale, bias):
        tab = "jt%d" % k
        gat = [lambda i=i: (agather("ob", src, tab, C if k == 2 else 0, i), add_piece(src, i) if i < 2 else None)
               for i in range(NCH)]
        eva = [lambda i=i: (evac_turned(dst, i) if k == 2 else evac(dst, i, scale, bias),
                            add_piece(src, i + 2) if i < 2 else None) for i in range(NCH)]
        return gat + eva

    def send_half(t):
        cp(ap("hs%d" % t), ap("ph", 0, C))
        exchange(t, ap("hr%d" % t), ap("hs%d" % t))

    for t in range(2):
        K = K0 + t
        now[0] = t
        na = NCH - SHARE[t]

        def bstep(k, i):
            vgather(ww[k + 1], ww[k], "jt%d" % k, C, i, "uu", A.max)
            if k < K - 1:
                rows = (0, "both")[t]
                dma(ap("uu", i * CH, (i + 1) * CH, row=rows), ap(ww[k + 1], i * CH, (i + 1) * CH, row=rows))

        if t == 0:
            x = "xa"
            first_list()
            mm(ap("pg", 0, C), ap("i1"), ap("cfr"), True, False)
            for i in range(NCH):
                vgather("ma", x, "own0", 0, i, "xc", A.max)
                agather("ob", x, "own0", 0, i)
                reduce_piece("pg", "zs", "ma", i, False)
                if i == 0:
                    cp(ap("own0", C, 2 * C), ap("ph", 0, C))
                    exchange(0, ap("par0", C, 2 * C), ap("own0", C, 2 * C))
                    iota(ap("w0"), [[-1, 16], [-16, C]], E - 1, 0, behind=[ap("own0", C, 2 * C)])
                    dma(ap("uu"), ap("w0"), "g")
            jconv(0)
            for h in range(4):
                add_turned(x, h)
            mm(ap("ph", 0, C), ap("i1"), ap("k1"), True, False)
            act(ap("zm"), ap("zs"), -1.0)
            act(ap("ze"), ap("zs"), col("ce"))
            for u in range(8):
                mm(ap("pg", 0, C), band("ze", 14 - 2 * u), ap("j0", u, E // 2, 8), False, False)
            for i in range(NCH):
                vgather("mb", x, "par0", 0, i, "xc", A.max)
                jstep(0, i)
                reduce_piece("ph", "zs", "mb", i, False)
            for i in range(NCH):
                vgather("ma", x, "par0", C, i, "xc", A.max)
                first_evac(x, i, -64.0, na)
                reduce_piece("ph", "zm", "ma", i, i == 3)
                if i == 1:
                    jconv(1)
            for i in range(NCH):
                vgather("mb", x, "own0", C, i, "xc", A.max)
                if i == 0:
                    send_half(0)
                    exchange(1, ap("par1"), ap("own0"))
                jstep(1, i, False)
                if i >= 1:
                    lists_piece(jw[2], i - 1, False)
                reduce_piece("pg", "zm", "mb", i, i == 3)
            lists_piece(jw[2], 3, False)
        else:
            x = "xb"
            nv = NCH - NS
            mm(ap("pg", 0, C), ap("i1"), ap("cfr"), True, False)
            mm(ap("ph", 0, C), ap("i1"), ap("k1"), True, False)
            parts = [scalar_gains(x, i) for i in range(nv, NCH)]
            for i in range(nv, NCH):
                agather("ob", x, "own0", 0, i)
            work = ([("mb", "par1", 0, i, "ph", "zs") for i in range(NCH)] + [("ma", "par1", C, i, "ph", "zm") for i in range(NCH)]
                    + [("mb", "own0", 0, i, "pg", "zs") for i in range(nv)] + [("ma", "own0", C, i, "pg", "zm") for i in range(nv)])
            for n, (m, tab, base, i, ps, z) in enumerate(work):
                vgather(m, x, tab, base, i, "xc", A.max)
                if n == 0 and parts:
                    parts[0][0]()
                    parts[0][1]()
                    if len(parts) > 1:
                        parts[1][0]()
                if n == PM[0]:
                    tt(ap("nw"), ap("bt"), ap("tk"), A.not_equal)
                    mm(ap("pj", 0, C), ap("p2"), ap("nw"), True, True)
                    mm(ap("pj", C, 2 * C), ap("p2"), ap("nw"), True, True)
                if n == PM[1]:
                    ts(ap("md"), ap("pj", 0, 2 * C), 0.0, None, A.is_equal)
                    tt(ap("td"), ap("md"), ap("ddig"), A.mult)
                    tt(ap("dig1"), ap("dig0"), ap("td"), A.add)
                    dma(ap("j0", row=0), ap("dig1", 0, C))
                    dma(ap("j0", row=1), ap("dig1", C, 2 * C))
                    mm(ap("pj", C, 2 * C), ap("i16"), ap("dig1", 0, C), True, False)
                    mm(ap("pj", C, 2 * C), ap("i1"), ap("dig1", C, 2 * C), False, True)
                    ts(ap("bi"), ap("bt"), 4096.0, None, A.mult)
                    ts(ap("vi"), ap("bi"), 1, 2047, A.arith_shift_right, A.bitwise_and)
                    cp(ap("vf"), ap("vi"))
                if n == PM[2]:
                    cp(ap("own1"), ap("pj", C, 2 * C))
                    if len(parts) > 1:
                        parts[1][1]()
                    act(ap("suf"), ap("pj", C, 2 * C))
                    for k in range(NCH):
                        agather("ob", x, "own1", 0, k)
                    for p in parts:
                        p[2]()
                if n == PM[3]:
                    first_list()
                    mm(ap("pj", 0, C), ap("sf"), ap("vf"), True, True)
                if n == PM[4]:
                    jconv(0)
                    tt(ap("eqt"), ap("pj", 0, C), ap("vf"), A.is_equal)
                    mm(ap("pg", 0, C), ap("ie"), ap("eqt"), False, False)
                if n == 8:
                    send_half(1)
                if n == PM[5]:
                    for h in range(4):
                        add_turned(x, h)
                if PM[6] <= n < PM[6] + 4:
                    jstep(0, n - PM[6])
                if PM[6] + 4 <= n < PM[6] + 8:
                    first_evac(x, n - PM[6] - 4, -64.0 - 2 * XOFF, na)
                if n == PM[7]:
                    jconv(1)
                reduce_piece(ps, z, m, i, n == 7 or n == len(work) - 1)
            for i in range(max(0, len(work) - PM[6] - 4), NCH):
                first_evac(x, i, -64.0 - 2 * XOFF, na)
        if t == 0:
            vgather("ab", "aa", "jt1", C, na, "ab", A.add)
            jconv(2)
        ts(ap("hpe"), ap("hr%d" % t), col("ch"), None, A.add)
        tt(ap("tk"), ap("pg", 0, C), ap("hpe"), A.add)
        tt(ap("bk"), ap("tk"), ap("efr"), A.max)
        dma(ap("w0", row=0), ap("bk"))
        dma(ap("uu", row=0), ap("bk"))
        if t == 0:
            mm(ap("ph"), ap("s1"), ap("dig0"), True, True)
            ts(ap("p2"), ap("yh", 0, 128), col("kf", 2), -4096.0, A.is_equal, A.mult)
            tt(ap("ddig"), ap("ph"), ap("dig0"), A.subtract)
        else:
            for i in range(NCH):
                jstep(1, i)
        for i in range(na):
            agather("ob", "aa", "jt1", C, i)
            add_piece("aa", i)
        for i in range(na + 1 - t, NCH):
            vgather("ab", "aa", "jt1", C, i, "ab", A.add)
        for i in range(na):
            evac("ab", i, 1.0, 0.0)
        a3 = astep(2, "ab", "aa", 1.0, 0.0)
        if t == 0:
            for i in range(NCH):
                bstep(0, i)
                jstep(2, i)
            for i in range(NCH):
                bstep(1, i)
                a3[i]()
            jconv(3)
            for k in (2, 3):
                for i in range(NCH):
                    bstep(k, i)
            dma(ap("bt"), ap("wb", row=0))
            rest = a3[4:] + astep(3, "aa", "xb", 1.0 / 16, 32.0 + XOFF - 0.46875)
            for n, f in enumerate(rest):
                f()
                if n >= 8:
                    dma(piece("xc", n - 8), piece("xb", n - 8), "g")
            act(ap("m1"), ap("i1"), -1.0)
            act(ap("i16"), ap("i1"), 16.0)
            act(ap("ie"), ap("i1"), -8192.0)
            act(ap("sf"), ap("s1"))
            continue
        act(col("cp"), col("kf", 1), 256.0)
        act(col("cdq"), col("cdp"), 256.0)
        act(ap("pos"), ap("cc"), 1.0, col("cp"))
        jconv(2)
        for i in range(NCH):
            bstep(0, i)
        dma(ap("w0", row=2), ap("suf"))
        for f in a3[:4]:
            f()
        for i in range(NCH):
            bstep(1, i)
            jstep(2, i)
        for f in a3[4:]:
            f()
        for i in range(NCH):
            bstep(2, i)
            if i == 1:
                jconv(3)
        b4 = (32.0 + XOFF - 0.484375) / 2
        a4 = astep(3, "aa", "af", 1.0 / 32, b4)
        for i in range(NCH):
            bstep(3, i)
            jstep(3, i)
        jconv(4)
        for f in a4[:6]:
            f()
        dma(piece("olab", 0), piece("af", 0), "g")
        dma(piece("olab", 1), piece("af", 1), "g")
        for f in a4[6:]:
            f()
        for i in (2, 3):
            evac("olab", i, 1.0 / 32, b4)
        for i in range(NCH):
            bstep(4, i)
        dma(ap("bt"), ap("wa", row=0))
        dma(ap("lt"), ap("wa", row=8))
        for i in range(TA):
            vgather("ab", "af", "jt4", 0, i, "olab", A.add)
            act(piece("aa", i), piece("ab", i), 1.0, -XOFF)
        tt(ap("nw"), ap("bt"), ap("tk"), A.not_equal)
        mm(ap("ph", 0, C), ap("sf"), ap("lt"), True, False)
        mm(ap("ph", 0, C), ap("p2"), ap("nw"), False, True)
        mm(ap("pg", 0, C), ap("p2"), ap("nw"), True, True)
        ts(ap("bi"), ap("bt"), 4096.0, None, A.mult)
        ts(ap("t1"), ap("pg", 0, C), 0.0, col("cdq"), A.is_equal, A.mult)
        tt(ap("zt"), ap("ph", 0, C), ap("lt"), A.max)
        dma(ap("wb", row=0), ap("zt"))
        dma((T.yx[:, 0:TA * CH], None), piece("aa", 0, TA), "g")
        tt(ap("t2"), ap("t1"), ap("pos"), A.add)
        ts(ap("loi"), ap("bi"), 15, None, A.bitwise_and)
        cp(ap("lsu"), ap("t2"))
        ts(ap("hii"), ap("bi"), 4, 255, A.arith_shift_right, A.bitwise_and)
        ts(ap("t3"), ap("loi"), 256.0, None, A.mult)
        tt(ap("t4"), ap("t3"), ap("hii"), A.add)
        cp(ap("llab"), ap("t4"))
        for i in range(NCH):
            agather("uu", "w0", "lsu", 0, i)
        for i in range(TA, NCH):
            vgather("ab", "af", "jt4", 0, i, "olab", A.add)
            if i > TA:
                ts(piece("aa", i - 1), piece("ab", i - 1), -XOFF, None, A.add)
                dma((T.yx[:, (i - 1) * CH:i * CH], None), piece("aa", i - 1), "g")
        dma((T.ysu[:], None), ap("uu", row=2))
        for i in range(NCH):
            if i < TL:
                w, f, d = ap("wb"), offs("llab", 0, i), piece("olab", i)
                op("v", lambda w=w, f=f, d=d: g.vector.tensor_scalar(d[0], w[0].indirect(f[0]), -1.0, float(E - 1), A.mult, A.add),
                   [w, f], [d], how="gather")
            else:
                agather("olab", "wb", "llab", 0, i, -1.0, float(E - 1))
            if i == 0:
                ts(piece("aa", 3), piece("ab", 3), -XOFF, None, A.add)
                dma((T.yx[:, 3 * CH:E], None), piece("aa", 3), "g")
        for i in (0, 2, 1, 3):
            dma((T.ylab[:, i * CH:(i + 1) * CH], None), ap("olab", i * CH, (i + 1) * CH, row=0))

    def meets(a, b):
        return a[1] < b[2] and b[1] < a[2] and (a[3] is None or b[3] is None or a[3] == b[3])

    hist = {}
    for n, o in enumerate(ops):
        deps = set()
        for reg in o["r"]:
            deps.update(m for m, r2, wr in hist.get(reg[0], []) if wr and meets(reg, r2))
        for reg in o["w"]:
            deps.update(m for m, r2, wr in hist.get(reg[0], []) if meets(reg, r2))
        if o["kind"] == "x":
            deps.add(n - 1)
        o["all"] = deps
        for reg in o["w"]:
            hist[reg[0]] = [h for h in hist.get(reg[0], []) if not (
                reg[1] <= h[1][1] and h[1][2] <= reg[2] and reg[3] in (None, h[1][3]) and o["full"])]
        for reg in o["r"]:
            hist.setdefault(reg[0], []).append((n, reg, False))
        for reg in o["w"]:
            hist.setdefault(reg[0], []).append((n, reg, True))
    after = [[] for _ in ops]
    for n, o in enumerate(ops):
        for m in o["all"]:
            after[m].append(n)
    waiting = [len(o["all"]) for o in ops]
    ready = [0.0] * len(ops)
    free = {q: 0.0 for q in ("v", "a", "p", "g", "s", None)}
    pool = {q: [] for q in free}
    for n, o in enumerate(ops):
        if not waiting[n]:
            pool[o["q"]].append(n)
    order = []
    while len(order) < len(ops):
        best = None
        for q in pool:
            if pool[q]:
                t0 = max(free[q], min(ready[n] for n in pool[q]))
                if best is None or t0 < best[0]:
                    best = (t0, q)
        t0, q = best
        n = max((k for k in pool[q] if ready[k] <= t0 + EST["look"]),
                key=lambda k: (ops[k]["busy"] < EST["small"] and q == "v", ops[k]["up"] - k))
        pool[q].remove(n)
        t0 = max(t0, ready[n])
        free[q] = t0 + ops[n]["busy"]
        order.append(n)
        for k in after[n]:
            ready[k] = max(ready[k], free[q] + (0.0 if ops[k]["q"] == q == "p" else ops[n]["late"]))
            waiting[k] -= 1
            if not waiting[k]:
                pool[ops[k]["q"]].append(k)
    place = {n: i for i, n in enumerate(order)}
    run = [ops[n] for n in order]
    seen = {}
    for o in run:
        if o["q"] is None:
            continue
        last = {}
        deps = []
        for m in o["all"]:
            p = ops[m]
            if p["kind"] == "r" or (p["q"] == "p" and o["q"] == "p"):
                continue
            if p["kind"] == "c":
                last[p["q"]] = max(last.get(p["q"], -1), place[m])
            else:
                deps.append(place[m])
        o["need"] = []
        for m in sorted(deps + list(last.values())):
            p = run[m]
            key = (o["q"], p["q"] if p["kind"] == "c" else p["token"][0])
            if seen.get(key, -1) < m:
                seen[key] = m
                o["need"].append(m)
                p["sig"] = True
    count = {"v": 0, "a": 0, "p": 0, "g": 0}
    final = {}
    for o in run:
        if o["kind"] == "c" and o["sig"]:
            count[o["q"]] += 1
            o["token"] = ("q" + o["q"], count[o["q"]])
        if o["token"]:
            final[o["token"][0]] = o["token"][1]
    for o in run:
        if o["q"] is None:
            continue
        for m in o["need"]:
            s, n = run[m]["token"]
            eng[o["q"]].wait_ge(T.sem[s], n)
        ins = o["fn"]()
        if o["kind"] == "d":
            ins.then_inc(T.sem[o["token"][0]], 16)
        elif o["kind"] == "c" and o["sig"]:
            ins.then_inc(T.sem[o["token"][0]], 1)
    final["left"] = left[0]
    for s in sorted(final):
        g.wait_ge(T.sem[s], final[s])
